import numpy as np
import ml_dtypes


def mxq(x, axis, fmt="e4m3"):
    dtype, down = {"e4m3": (ml_dtypes.float8_e4m3fn, 7), "e5m2": (ml_dtypes.float8_e5m2, 14)}[fmt]
    v = np.moveaxis(np.asarray(x, np.float32).astype(ml_dtypes.bfloat16).astype(np.float64), axis, -1)
    blocks = v.reshape(v.shape[:-1] + (-1, 32))
    amax = np.abs(blocks).max(-1, keepdims=True)
    byte = np.maximum(np.where(amax > 0, np.frexp(amax)[1] - 1 + 127, 0) - down, 1)
    scale = np.exp2(byte - 127.0)
    codes = (blocks / scale).astype(np.float32).astype(dtype).astype(np.float64)
    return np.moveaxis((codes * scale).reshape(v.shape), -1, axis)


WIDE = False


def mx_kscale(k):
    if not WIDE:
        return np.ones(k)
    levels = np.array([10, -10, 5, -5, 0])
    if k % 512:
        return np.exp2(np.random.permutation(np.resize(levels, k // 32))).repeat(32)
    a = np.empty((k // 512, 16))
    for p in range(k // 512):
        a[p, :8] = np.random.permutation(np.resize(levels, 8))
        for g in range(8):
            far = levels[np.abs(levels - a[p, g]) >= 10]
            a[p, g + 8] = far[np.random.randint(len(far))]
    return np.exp2(a.ravel()).repeat(32)


def f64(x):
    return np.asarray(x).astype(np.float64)


def striped(idx):
    return np.tile(np.asarray(idx).reshape(-1, 16).T, (8, 1)).astype(np.uint16)


def unstriped(offs):
    return offs[:16].T.reshape(-1).astype(np.int64)


E2M1 = np.array([0.0, 0.5, 1.0, 1.5, 2.0, 3.0, 4.0, 6.0, -0.0, -0.5, -1.0, -1.5, -2.0, -3.0, -4.0, -6.0])


def pack_weight(w, fmt):
    k, n = w.shape
    w = f64(np.asarray(w, np.float32).astype(ml_dtypes.bfloat16)).reshape(k // 32, 32, n)
    amax = np.abs(w).max(1)
    if fmt == "e4m3":
        byte = np.frexp(amax)[1] - 1 + 127 - 7
    else:
        mant, ex = np.frexp(amax / 6.0)
        byte = np.where(mant > 0.5, ex, ex - 1) + 127
    byte = np.clip(np.where(amax > 0, byte, 1), 1, 254)
    scaled = (w * np.exp2(127.0 - byte)[:, None, :]).reshape(k, n).astype(np.float32)
    by_word = np.ascontiguousarray(scaled.reshape(k // 512, 128, 4, n).transpose(0, 1, 3, 2))
    if fmt == "e4m3":
        words = by_word.astype(ml_dtypes.float8_e4m3fn).view(np.uint8)
    else:
        c = by_word.astype(ml_dtypes.float4_e2m1fn).view(np.uint8) & 0xF
        words = (c[..., 0::2] | (c[..., 1::2] << 4)).reshape(k // 512, 128, 2 * n)
    return np.ascontiguousarray(words), np.ascontiguousarray(byte.astype(np.uint8).reshape(k // 512, 16, n))


def unpack_weight(words, scales, fmt):
    g, _, n = scales.shape
    words = np.ascontiguousarray(words).reshape(g, 128, n, -1)
    if fmt == "e4m3":
        vals = words.view(ml_dtypes.float8_e4m3fn).astype(np.float64)
    else:
        nib = np.empty((g, 128, n, 4), np.uint8)
        nib[..., 0::2] = words & 0xF
        nib[..., 1::2] = words >> 4
        vals = E2M1[nib]
    vals = vals * np.repeat(np.exp2(scales.astype(np.float64) - 127.0), 8, axis=1)[..., None]
    return vals.transpose(0, 1, 3, 2).reshape(g * 512, n)


K, T, J, L, N = 1024, 2048, 512, 512, 512


def setup_inputs():
    n = np.random.standard_normal
    idx = np.random.permutation(T)[:J]
    fk = mx_kscale(K)
    fl = mx_kscale(L)
    xtp = pack_weight(n((K, T)) / fk[:, None], "e2m1")
    cxp = pack_weight(n((L, J)) / fl[:, None], "e4m3")
    wcp = pack_weight(n((L, N)) * 1 / np.sqrt(L) * fl[:, None], "e2m1")
    return {
        "xt_words": xtp[0],
        "xt_scales": xtp[1],
        "w": (n((K, N)) * 1 / np.sqrt(K) * fk[:, None]).astype(np.float32),
        "cx_words": cxp[0],
        "cx_scales": cxp[1],
        "wc_words": wcp[0],
        "wc_scales": wcp[1],
        "ta": (np.random.uniform(0.5, 2.0, (N, 1))).astype(np.float32),
        "tb": (np.random.uniform(-1.0, 1.0, (N, 1))).astype(np.float32),
        "td": (np.random.uniform(-0.5, 0.5, (N, 1))).astype(np.float32),
        "offs": striped(idx),
    }


def reference(xt_words, xt_scales, w, cx_words, cx_scales, wc_words, wc_scales, ta, tb, td, offs):
    idx = unstriped(offs)
    xtu = unpack_weight(xt_words, xt_scales, "e2m1")
    cxu = unpack_weight(cx_words, cx_scales, "e4m3")
    wcu = unpack_weight(wc_words, wc_scales, "e2m1")
    wq = mxq(f64(w), 0, "e4m3")
    xtidxg = xtu[:, idx]
    z = wq.T @ xtidxg
    za = np.pad(z, ((0, 0), (1, 0)))[:, :J]
    zb = np.pad(z, ((0, 0), (2, 0)))[:, :J]
    s = wcu.T @ cxu
    y = f64(ta) * z + f64(tb) * za + f64(td) * zb + s
    return y

@@ -1,0 +1,170 @@
+from contextlib import ExitStack
+
+import concourse.mybir as mybir
+from concourse.masks import make_identity
+
+K, T, J, L, N = 1024, 2048, 512, 512, 512
+FLOPS = 2 * (K + L) * N * J
+
+F32 = mybir.dt.float32
+BF16 = mybir.dt.bfloat16
+I32 = mybir.dt.int32
+U32 = mybir.dt.uint32
+U16 = mybir.dt.uint16
+U8 = mybir.dt.uint8
+FP8X4 = mybir.dt.float8_e4m3fn_x4
+FP4X4 = mybir.dt.float4_e2m1fn_x4
+MULT = mybir.AluOpType.mult
+ADD = mybir.AluOpType.add
+COPY = mybir.ActivationFunctionType.Copy
+
+P = 128
+PACK = 4
+PASSES = K // (P * PACK)
+CHUNKS = ((0,), (1, 2), (3,))
+EARLY_TILES = (0, 1)
+HALVES = (0, J // 2, J)
+
+
+def tile_list_lagged_taps_kernel(tc, xt_words, xt_scales, w, cx_words, cx_scales, wc_words, wc_scales, ta, tb, td, offs, out):
+    nc = tc.nc
+    with ExitStack() as ctx:
+        keep = ctx.enter_context(tc.tile_pool(name="keep", bufs=1))
+        psum = ctx.enter_context(tc.psum_pool(name="psum", bufs=1))
+
+        offsets = keep.tile([P, J // 16], U16, name="offsets")
+        nc.sync.dma_start(offsets[:], offs)
+
+        xs = keep.tile([P, T], U8, name="xs", align_bytes=64)
+        cs = keep.tile([P, J], U8, name="cs", align_bytes=64)
+        ws = keep.tile([P, N], U8, name="ws", align_bytes=64)
+        gs = [keep.tile([P, J], U8, name="gs%d" % a, align_bytes=64) for a in range(PASSES)]
+        tap_rows = keep.tile([P, P], F32, name="tap_rows")
+        ident = keep.tile([P, P], F32, name="ident")
+        nc.gpsimd.memset(xs[:].bitcast(I32), 0)
+        nc.gpsimd.memset(tap_rows[:], 0.0)
+        nc.vector.memset(gs[1][:].bitcast(I32), 0)
+        nc.vector.memset(ws[:].bitcast(I32), 0)
+        nc.vector.memset(cs[:].bitcast(I32), 0)
+
+        xs_src = xt_scales.bitcast(I32)
+        for q in range(4):
+            nc.sync.dma_start(xs[32 * q : 32 * q + 8, :].bitcast(I32), xs_src[:, 4 * q : 4 * q + 4, :])
+        for i, tap_in in enumerate((ta, tb, td)):
+            nc.gpsimd.dma_start(tap_rows[4 * i : 4 * i + 4, :], tap_in.rearrange("(t p) o -> t (p o)", p=P))
+        make_identity(nc, ident[:])
+
+        xw = [keep.tile([P, T], U16, name="xw%d" % a, align_bytes=64) for a in range(PASSES)]
+        raw = {}
+
+        def load_w(c, a):
+            tiles = CHUNKS[c]
+            raw[c, a] = keep.tile([P, PACK, P * len(tiles)], F32, name="raw%d%d" % (c, a))
+            rows = w[a * 512 : (a + 1) * 512, P * tiles[0] : P * (tiles[-1] + 1)]
+            nc.sync.dma_start(raw[c, a][:], rows.rearrange("(p t) n -> p t n", t=PACK))
+
+        for a in range(PASSES):
+            nc.sync.dma_start(xw[a][:].bitcast(I32), xt_words[a].bitcast(I32))
+            load_w(0, a)
+        load_w(1, 0)
+        load_w(1, 1)
+        cw = keep.tile([P, J], U32, name="cw", align_bytes=64)
+        ww = keep.tile([P, 2 * N], U8, name="ww", align_bytes=64)
+        nc.sync.dma_start(cw[:].bitcast(I32), cx_words[0].rearrange("p n t -> p (n t)").bitcast(I32))
+        nc.sync.dma_start(ww[:].bitcast(I32), wc_words[0].bitcast(I32))
+        load_w(2, 0)
+        load_w(2, 1)
+        for q in range(4):
+            nc.sync.dma_start(cs[32 * q : 32 * q + 4, :].bitcast(I32), cx_scales[0, 4 * q : 4 * q + 4, :].bitcast(I32))
+
+        gw = [keep.tile([P, J], U16, name="gw%d" % a, align_bytes=64) for a in range(PASSES)]
+        nc.vector.tensor_copy(gs[0][:], xs[:].indirect(offsets[:]))
+        nc.gpsimd.dma_start(gs[1][0:100, :].bitcast(I32), gs[0][4:104, :].bitcast(I32))
+        for q in range(4):
+            nc.gpsimd.dma_start(ws[32 * q : 32 * q + 4, :].bitcast(I32), wc_scales[0, 4 * q : 4 * q + 4, :].bitcast(I32))
+        for a in range(PASSES):
+            nc.vector.tensor_copy(gw[a][:], xw[a][:].indirect(offsets[:]))
+
+        tap_ps = psum.tile([P, P], F32, name="tap_ps", tag="s3")
+        nc.tensor.transpose(tap_ps[:], tap_rows[:], ident[:])
+        taps = keep.tile([P, 12], F32, name="taps")
+        nc.scalar.copy(taps[:], tap_ps[:, 0:12])
+
+        z, s, y = {}, {}, {}
+
+        def features(c, a):
+            tiles = CHUNKS[c]
+            width = P * len(tiles)
+            grouped = keep.tile([P, width * PACK], BF16, name="grouped%d%d" % (c, a), align_bytes=64)
+            nc.scalar.copy(
+                grouped[:].rearrange("p (c i t) -> p c t i", i=4, t=PACK),
+                raw[c, a][:].rearrange("p t (c i) -> p c t i", i=4),
+            )
+            codes = keep.tile([P, width], U32, name="codes%d%d" % (c, a), align_bytes=64)
+            plane = keep.tile([P, width], U8, name="plane%d%d" % (c, a), align_bytes=64)
+            nc.vector.quantize_mx(out=codes[:].bitcast(FP8X4), scales=plane[:], in_=grouped[:])
+            for e, t in enumerate(tiles):
+                if a == 0:
+                    z[t] = psum.tile([P, J], F32, name="z%d" % t)
+                nc.tensor.matmul_mx(
+                    out=z[t][:],
+                    lhsT=codes[:, P * e : P * (e + 1)].bitcast(FP8X4),
+                    lhsT_scale=plane[:, P * e : P * (e + 1)],
+                    rhs=gw[a][:].bitcast(FP4X4),
+                    rhs_scale=gs[a][:],
+                    start=(a == 0),
+                    stop=(a == PASSES - 1),
+                )
+
+        def context(t):
+            s[t] = psum.tile([P, J], F32, name="s%d" % t, tag="s%d" % t)
+            nc.tensor.matmul_mx(
+                out=s[t][:],
+                lhsT=ww[:, 2 * P * t : 2 * P * (t + 1)].bitcast(FP4X4),
+                lhsT_scale=ws[:, P * t : P * (t + 1)],
+                rhs=cw[:].bitcast(FP8X4),
+                rhs_scale=cs[:],
+                start=True,
+                stop=True,
+            )
+
+        def tap_of(t, lag):
+            return taps[:, 4 * lag + t : 4 * lag + t + 1]
+
+        def add_tap(t, lag):
+            for lo, hi in zip(HALVES, HALVES[1:]):
+                lo = max(lo, lag)
+                nc.vector.scalar_tensor_tensor(y[t][:, lo:hi], z[t][:, lo - lag : hi - lag], tap_of(t, lag), y[t][:, lo:hi], MULT, ADD)
+
+        def begin(t):
+            y[t] = keep.tile([P, J], F32, name="y%d" % t)
+            if t in EARLY_TILES:
+                nc.scalar.activation(y[t][:], z[t][:], COPY, scale=tap_of(t, 0))
+            else:
+                context(t)
+                nc.scalar.copy(y[t][:], s[t][:])
+                add_tap(t, 0)
+            add_tap(t, 1)
+            add_tap(t, 2)
+
+        def finish(t):
+            if t in EARLY_TILES:
+                context(t)
+                for lo, hi in zip(HALVES, HALVES[1:]):
+                    nc.vector.tensor_tensor(y[t][:, lo:hi], s[t][:, lo:hi], y[t][:, lo:hi], ADD)
+            nc.sync.dma_start(out[P * t : P * (t + 1), :], y[t][:])
+
+        features(0, 0)
+        features(0, 1)
+        begin(0)
+        features(1, 0)
+        features(1, 1)
+        begin(1)
+        finish(0)
+        finish(1)
+        features(2, 0)
+        features(2, 1)
+        begin(2)
+        finish(2)
+        begin(3)
+        finish(3)

@@ -21,9 +21,7 @@ COPY = mybir.ActivationFunctionType.Copy
 P = 128
 PACK = 4
 PASSES = K // (P * PACK)
-CHUNKS = ((0,), (1, 2), (3,))
-EARLY_TILES = (0, 1)
-HALVES = (0, J // 2, J)
+TILES = N // P
 
 
 def tile_list_lagged_taps_kernel(tc, xt_words, xt_scales, w, cx_words, cx_scales, wc_words, wc_scales, ta, tb, td, offs, out):
@@ -35,77 +33,81 @@ def tile_list_lagged_taps_kernel(tc, xt_words, xt_scales, w, cx_words, cx_scales
         offsets = keep.tile([P, J // 16], U16, name="offsets")
         nc.sync.dma_start(offsets[:], offs)
 
-        xs = keep.tile([P, T], U8, name="xs", align_bytes=64)
+        xs = keep.tile([P, PASSES * T], U8, name="xs", align_bytes=64)
         cs = keep.tile([P, J], U8, name="cs", align_bytes=64)
         ws = keep.tile([P, N], U8, name="ws", align_bytes=64)
         gs = [keep.tile([P, J], U8, name="gs%d" % a, align_bytes=64) for a in range(PASSES)]
         tap_rows = keep.tile([P, P], F32, name="tap_rows")
         ident = keep.tile([P, P], F32, name="ident")
-        nc.gpsimd.memset(xs[:].bitcast(I32), 0)
-        nc.gpsimd.memset(tap_rows[:], 0.0)
-        nc.vector.memset(gs[1][:].bitcast(I32), 0)
+        nc.gpsimd.memset(xs[:, 0:T].bitcast(I32), 0)
+        nc.vector.memset(xs[:, T : 2 * T].bitcast(I32), 0)
+        make_identity(nc, ident[:])
+        nc.vector.memset(tap_rows[:], 0.0)
         nc.vector.memset(ws[:].bitcast(I32), 0)
         nc.vector.memset(cs[:].bitcast(I32), 0)
 
-        xs_src = xt_scales.bitcast(I32)
-        for q in range(4):
-            nc.sync.dma_start(xs[32 * q : 32 * q + 8, :].bitcast(I32), xs_src[:, 4 * q : 4 * q + 4, :])
-        for i, tap_in in enumerate((ta, tb, td)):
-            nc.gpsimd.dma_start(tap_rows[4 * i : 4 * i + 4, :], tap_in.rearrange("(t p) o -> t (p o)", p=P))
-        make_identity(nc, ident[:])
+        def load_plane(plane, scales):
+            for q in range(4):
+                nc.sync.dma_start(plane[32 * q : 32 * q + 4, :].bitcast(I32), scales[0, 4 * q : 4 * q + 4, :].bitcast(I32))
 
         xw = [keep.tile([P, T], U16, name="xw%d" % a, align_bytes=64) for a in range(PASSES)]
         raw = {}
 
-        def load_w(c, a):
-            tiles = CHUNKS[c]
-            raw[c, a] = keep.tile([P, PACK, P * len(tiles)], F32, name="raw%d%d" % (c, a))
+        def load_w(tiles, a):
             rows = w[a * 512 : (a + 1) * 512, P * tiles[0] : P * (tiles[-1] + 1)]
-            nc.sync.dma_start(raw[c, a][:], rows.rearrange("(p t) n -> p t n", t=PACK))
+            loaded = keep.tile([P, PACK, P * len(tiles)], F32, name="raw%d%d" % (tiles[0], a), tag="raw%d%d" % (tiles[0], a))
+            nc.sync.dma_start(loaded[:], rows.rearrange("(p t) n -> p t n", t=PACK))
+            for e, t in enumerate(tiles):
+                raw[t, a] = (loaded, P * e)
 
-        for a in range(PASSES):
-            nc.sync.dma_start(xw[a][:].bitcast(I32), xt_words[a].bitcast(I32))
-            load_w(0, a)
-        load_w(1, 0)
-        load_w(1, 1)
         cw = keep.tile([P, J], U32, name="cw", align_bytes=64)
         ww = keep.tile([P, 2 * N], U8, name="ww", align_bytes=64)
+        xs_src = xt_scales.bitcast(I32)
+        nc.sync.dma_start(xw[0][:].bitcast(I32), xt_words[0].bitcast(I32))
+        nc.sync.dma_start(xw[1][:].bitcast(I32), xt_words[1].bitcast(I32))
+        for q in range(4):
+            nc.sync.dma_start(
+                xs[32 * q : 32 * q + 4, :].bitcast(I32).rearrange("r (a c) -> r a c", a=PASSES),
+                xs_src[:, 4 * q : 4 * q + 4, :].rearrange("a r c -> r a c"),
+            )
+        load_w((0, 1), 0)
+        load_w((0, 1), 1)
+        for i, tap_in in enumerate((ta, tb, td)):
+            nc.sync.dma_start(tap_rows[4 * i : 4 * i + 4, :], tap_in.rearrange("(t p) o -> t (p o)", p=P))
+        load_w((2, 3), 0)
+        load_w((2, 3), 1)
         nc.sync.dma_start(cw[:].bitcast(I32), cx_words[0].rearrange("p n t -> p (n t)").bitcast(I32))
         nc.sync.dma_start(ww[:].bitcast(I32), wc_words[0].bitcast(I32))
-        load_w(2, 0)
-        load_w(2, 1)
-        for q in range(4):
-            nc.sync.dma_start(cs[32 * q : 32 * q + 4, :].bitcast(I32), cx_scales[0, 4 * q : 4 * q + 4, :].bitcast(I32))
+        load_plane(cs, cx_scales)
+        load_plane(ws, wc_scales)
 
         gw = [keep.tile([P, J], U16, name="gw%d" % a, align_bytes=64) for a in range(PASSES)]
-        nc.vector.tensor_copy(gs[0][:], xs[:].indirect(offsets[:]))
-        nc.gpsimd.dma_start(gs[1][0:100, :].bitcast(I32), gs[0][4:104, :].bitcast(I32))
-        for q in range(4):
-            nc.gpsimd.dma_start(ws[32 * q : 32 * q + 4, :].bitcast(I32), wc_scales[0, 4 * q : 4 * q + 4, :].bitcast(I32))
         for a in range(PASSES):
             nc.vector.tensor_copy(gw[a][:], xw[a][:].indirect(offsets[:]))
+        for a in range(PASSES):
+            nc.vector.tensor_copy(gs[a][:], xs[:, a * T : (a + 1) * T].indirect(offsets[:]))
 
         tap_ps = psum.tile([P, P], F32, name="tap_ps", tag="s3")
         nc.tensor.transpose(tap_ps[:], tap_rows[:], ident[:])
         taps = keep.tile([P, 12], F32, name="taps")
         nc.scalar.copy(taps[:], tap_ps[:, 0:12])
 
-        z, s, y = {}, {}, {}
+        z, s = {}, {}
 
-        def features(c, a):
-            tiles = CHUNKS[c]
+        def features(tiles, a, copy=nc.scalar.copy):
+            loaded, first = raw[tiles[0], a]
             width = P * len(tiles)
-            grouped = keep.tile([P, width * PACK], BF16, name="grouped%d%d" % (c, a), align_bytes=64)
-            nc.scalar.copy(
+            grouped = keep.tile([P, width * PACK], BF16, name="grouped%d%d" % (tiles[0], a), align_bytes=64)
+            copy(
                 grouped[:].rearrange("p (c i t) -> p c t i", i=4, t=PACK),
-                raw[c, a][:].rearrange("p t (c i) -> p c t i", i=4),
+                loaded[:, :, first : first + width].rearrange("p t (c i) -> p c t i", i=4),
             )
-            codes = keep.tile([P, width], U32, name="codes%d%d" % (c, a), align_bytes=64)
-            plane = keep.tile([P, width], U8, name="plane%d%d" % (c, a), align_bytes=64)
+            codes = keep.tile([P, width], U32, name="codes%d%d" % (tiles[0], a), align_bytes=64)
+            plane = keep.tile([P, width], U8, name="plane%d%d" % (tiles[0], a), align_bytes=64)
             nc.vector.quantize_mx(out=codes[:].bitcast(FP8X4), scales=plane[:], in_=grouped[:])
             for e, t in enumerate(tiles):
                 if a == 0:
-                    z[t] = psum.tile([P, J], F32, name="z%d" % t)
+                    z[t] = psum.tile([P, J], F32, name="z%d" % t, tag="z%d" % t)
                 nc.tensor.matmul_mx(
                     out=z[t][:],
                     lhsT=codes[:, P * e : P * (e + 1)].bitcast(FP8X4),
@@ -129,42 +131,32 @@ def tile_list_lagged_taps_kernel(tc, xt_words, xt_scales, w, cx_words, cx_scales
             )
 
         def tap_of(t, lag):
-            return taps[:, 4 * lag + t : 4 * lag + t + 1]
+            return taps[:, TILES * lag + t : TILES * lag + t + 1]
+
+        def first_tap(t):
+            nc.scalar.activation(y[:, t, :], z[t][:], COPY, scale=tap_of(t, 0))
 
         def add_tap(t, lag):
-            for lo, hi in zip(HALVES, HALVES[1:]):
-                lo = max(lo, lag)
-                nc.vector.scalar_tensor_tensor(y[t][:, lo:hi], z[t][:, lo - lag : hi - lag], tap_of(t, lag), y[t][:, lo:hi], MULT, ADD)
+            nc.vector.scalar_tensor_tensor(y[:, t, lag:J], z[t][:, 0 : J - lag], tap_of(t, lag), y[:, t, lag:J], MULT, ADD)
 
-        def begin(t):
-            y[t] = keep.tile([P, J], F32, name="y%d" % t)
-            if t in EARLY_TILES:
-                nc.scalar.activation(y[t][:], z[t][:], COPY, scale=tap_of(t, 0))
-            else:
-                context(t)
-                nc.scalar.copy(y[t][:], s[t][:])
-                add_tap(t, 0)
-            add_tap(t, 1)
-            add_tap(t, 2)
+        def finish(t, lo=0, hi=J):
+            nc.vector.tensor_tensor(y[:, t, lo:hi], s[t][:, lo:hi], y[:, t, lo:hi], ADD)
+            nc.sync.dma_start(out[P * t : P * (t + 1), lo:hi], y[:, t, lo:hi])
 
-        def finish(t):
-            if t in EARLY_TILES:
-                context(t)
-                for lo, hi in zip(HALVES, HALVES[1:]):
-                    nc.vector.tensor_tensor(y[t][:, lo:hi], s[t][:, lo:hi], y[t][:, lo:hi], ADD)
-            nc.sync.dma_start(out[P * t : P * (t + 1), :], y[t][:])
-
-        features(0, 0)
-        features(0, 1)
-        begin(0)
-        features(1, 0)
-        features(1, 1)
-        begin(1)
-        finish(0)
-        finish(1)
-        features(2, 0)
-        features(2, 1)
-        begin(2)
-        finish(2)
-        begin(3)
-        finish(3)
+        features((0, 1), 0)
+        features((0, 1), 1)
+        features((2, 3), 0)
+        features((2, 3), 1, copy=nc.vector.tensor_copy)
+        y = keep.tile([P, TILES, J], F32, name="y", tag="raw20")
+        for pair in ((0, 1), (2, 3)):
+            for t in pair:
+                first_tap(t)
+            for lag in (1, 2):
+                for t in pair:
+                    add_tap(t, lag)
+        for t in range(TILES):
+            context(t)
+        for t in range(TILES - 1):
+            finish(t)
+        finish(3, 0, J // 2)
+        finish(3, J // 2, J)

@@ -47,8 +47,8 @@ def tile_list_lagged_taps_kernel(tc, xt_words, xt_scales, w, cx_words, cx_scales
         nc.vector.memset(cs[:].bitcast(I32), 0)
 
         def load_plane(plane, scales):
-            for q in range(4):
-                nc.sync.dma_start(plane[32 * q : 32 * q + 4, :].bitcast(I32), scales[0, 4 * q : 4 * q + 4, :].bitcast(I32))
+            for r in range(4):
+                nc.sync.dma_start(plane[r:P:32, :].bitcast(I32), scales[0, r:16:4, :].bitcast(I32))
 
         xw = [keep.tile([P, T], U16, name="xw%d" % a, align_bytes=64) for a in range(PASSES)]
         raw = {}
@@ -65,10 +65,10 @@ def tile_list_lagged_taps_kernel(tc, xt_words, xt_scales, w, cx_words, cx_scales
         xs_src = xt_scales.bitcast(I32)
         nc.sync.dma_start(xw[0][:].bitcast(I32), xt_words[0].bitcast(I32))
         nc.sync.dma_start(xw[1][:].bitcast(I32), xt_words[1].bitcast(I32))
-        for q in range(4):
+        for r in range(4):
             nc.sync.dma_start(
-                xs[32 * q : 32 * q + 4, :].bitcast(I32).rearrange("r (a c) -> r a c", a=PASSES),
-                xs_src[:, 4 * q : 4 * q + 4, :].rearrange("a r c -> r a c"),
+                xs[r:P:32, :].bitcast(I32).rearrange("q (a c) -> q a c", a=PASSES),
+                xs_src[:, r:16:4, :].rearrange("a q c -> q a c"),
             )
         load_w((0, 1), 0)
         load_w((0, 1), 1)
@@ -156,7 +156,11 @@ def tile_list_lagged_taps_kernel(tc, xt_words, xt_scales, w, cx_words, cx_scales
                     add_tap(t, lag)
         for t in range(TILES):
             context(t)
-        for t in range(TILES - 1):
-            finish(t)
+        for t in (0, 1):
+            aside = keep.tile([P, J], F32, name="aside%d" % t)
+            nc.scalar.copy(aside[:], s[t][:])
+            nc.gpsimd.tensor_tensor(y[:, t, :], y[:, t, :], aside[:], ADD)
+            nc.scalar.dma_start(out[P * t : P * (t + 1), :], y[:, t, :])
+        finish(2)
         finish(3, 0, J // 2)
         finish(3, J // 2, J)

from contextlib import ExitStack

import concourse.mybir as mybir
from concourse.masks import make_identity

K, T, J, L, N = 1024, 2048, 512, 512, 512
FLOPS = 2 * (K + L) * N * J

F32 = mybir.dt.float32
BF16 = mybir.dt.bfloat16
I32 = mybir.dt.int32
U32 = mybir.dt.uint32
U16 = mybir.dt.uint16
U8 = mybir.dt.uint8
FP8X4 = mybir.dt.float8_e4m3fn_x4
FP4X4 = mybir.dt.float4_e2m1fn_x4
MULT = mybir.AluOpType.mult
ADD = mybir.AluOpType.add
COPY = mybir.ActivationFunctionType.Copy

P = 128
PACK = 4
PASSES = K // (P * PACK)
TILES = N // P


def tile_list_lagged_taps_kernel(tc, xt_words, xt_scales, w, cx_words, cx_scales, wc_words, wc_scales, ta, tb, td, offs, out):
    nc = tc.nc
    with ExitStack() as ctx:
        keep = ctx.enter_context(tc.tile_pool(name="keep", bufs=1))
        psum = ctx.enter_context(tc.psum_pool(name="psum", bufs=1))

        offsets = keep.tile([P, J // 16], U16, name="offsets")
        nc.sync.dma_start(offsets[:], offs)

        xs = keep.tile([P, PASSES * T], U8, name="xs", align_bytes=64)
        cs = keep.tile([P, J], U8, name="cs", align_bytes=64)
        ws = keep.tile([P, N], U8, name="ws", align_bytes=64)
        gs = [keep.tile([P, J], U8, name="gs%d" % a, align_bytes=64) for a in range(PASSES)]
        tap_rows = keep.tile([P, P], F32, name="tap_rows")
        ident = keep.tile([P, P], F32, name="ident")
        nc.gpsimd.memset(xs[:, 0:T].bitcast(I32), 0)
        nc.vector.memset(xs[:, T : 2 * T].bitcast(I32), 0)
        make_identity(nc, ident[:])
        nc.vector.memset(tap_rows[:], 0.0)
        nc.vector.memset(ws[:].bitcast(I32), 0)
        nc.vector.memset(cs[:].bitcast(I32), 0)

        def load_plane(plane, scales):
            for r in range(4):
                nc.sync.dma_start(plane[r:P:32, :].bitcast(I32), scales[0, r:16:4, :].bitcast(I32))

        xw = [keep.tile([P, T], U16, name="xw%d" % a, align_bytes=64) for a in range(PASSES)]
        raw = {}

        def load_w(tiles, a):
            rows = w[a * 512 : (a + 1) * 512, P * tiles[0] : P * (tiles[-1] + 1)]
            loaded = keep.tile([P, PACK, P * len(tiles)], F32, name="raw%d%d" % (tiles[0], a), tag="raw%d%d" % (tiles[0], a))
            nc.sync.dma_start(loaded[:], rows.rearrange("(p t) n -> p t n", t=PACK))
            for e, t in enumerate(tiles):
                raw[t, a] = (loaded, P * e)

        cw = keep.tile([P, J], U32, name="cw", align_bytes=64)
        ww = keep.tile([P, 2 * N], U8, name="ww", align_bytes=64)
        xs_src = xt_scales.bitcast(I32)
        nc.sync.dma_start(xw[0][:].bitcast(I32), xt_words[0].bitcast(I32))
        nc.sync.dma_start(xw[1][:].bitcast(I32), xt_words[1].bitcast(I32))
        for r in range(4):
            nc.sync.dma_start(
                xs[r:P:32, :].bitcast(I32).rearrange("q (a c) -> q a c", a=PASSES),
                xs_src[:, r:16:4, :].rearrange("a q c -> q a c"),
            )
        load_w((0, 1), 0)
        load_w((0, 1), 1)
        for i, tap_in in enumerate((ta, tb, td)):
            nc.sync.dma_start(tap_rows[4 * i : 4 * i + 4, :], tap_in.rearrange("(t p) o -> t (p o)", p=P))
        load_w((2, 3), 0)
        load_w((2, 3), 1)
        nc.sync.dma_start(cw[:].bitcast(I32), cx_words[0].rearrange("p n t -> p (n t)").bitcast(I32))
        nc.sync.dma_start(ww[:].bitcast(I32), wc_words[0].bitcast(I32))
        load_plane(cs, cx_scales)
        load_plane(ws, wc_scales)

        gw = [keep.tile([P, J], U16, name="gw%d" % a, align_bytes=64) for a in range(PASSES)]
        for a in range(PASSES):
            nc.vector.tensor_copy(gw[a][:], xw[a][:].indirect(offsets[:]))
        for a in range(PASSES):
            nc.vector.tensor_copy(gs[a][:], xs[:, a * T : (a + 1) * T].indirect(offsets[:]))

        tap_ps = psum.tile([P, P], F32, name="tap_ps", tag="s3")
        nc.tensor.transpose(tap_ps[:], tap_rows[:], ident[:])
        taps = keep.tile([P, 12], F32, name="taps")
        nc.scalar.copy(taps[:], tap_ps[:, 0:12])

        z, s = {}, {}

        def features(tiles, a, copy=nc.scalar.copy):
            loaded, first = raw[tiles[0], a]
            width = P * len(tiles)
            grouped = keep.tile([P, width * PACK], BF16, name="grouped%d%d" % (tiles[0], a), align_bytes=64)
            copy(
                grouped[:].rearrange("p (c i t) -> p c t i", i=4, t=PACK),
                loaded[:, :, first : first + width].rearrange("p t (c i) -> p c t i", i=4),
            )
            codes = keep.tile([P, width], U32, name="codes%d%d" % (tiles[0], a), align_bytes=64)
            plane = keep.tile([P, width], U8, name="plane%d%d" % (tiles[0], a), align_bytes=64)
            nc.vector.quantize_mx(out=codes[:].bitcast(FP8X4), scales=plane[:], in_=grouped[:])
            for e, t in enumerate(tiles):
                if a == 0:
                    z[t] = psum.tile([P, J], F32, name="z%d" % t, tag="z%d" % t)
                nc.tensor.matmul_mx(
                    out=z[t][:],
                    lhsT=codes[:, P * e : P * (e + 1)].bitcast(FP8X4),
                    lhsT_scale=plane[:, P * e : P * (e + 1)],
                    rhs=gw[a][:].bitcast(FP4X4),
                    rhs_scale=gs[a][:],
                    start=(a == 0),
                    stop=(a == PASSES - 1),
                )

        def context(t):
            s[t] = psum.tile([P, J], F32, name="s%d" % t, tag="s%d" % t)
            nc.tensor.matmul_mx(
                out=s[t][:],
                lhsT=ww[:, 2 * P * t : 2 * P * (t + 1)].bitcast(FP4X4),
                lhsT_scale=ws[:, P * t : P * (t + 1)],
                rhs=cw[:].bitcast(FP8X4),
                rhs_scale=cs[:],
                start=True,
                stop=True,
            )

        def tap_of(t, lag):
            return taps[:, TILES * lag + t : TILES * lag + t + 1]

        def first_tap(t):
            nc.scalar.activation(y[:, t, :], z[t][:], COPY, scale=tap_of(t, 0))

        def add_tap(t, lag):
            nc.vector.scalar_tensor_tensor(y[:, t, lag:J], z[t][:, 0 : J - lag], tap_of(t, lag), y[:, t, lag:J], MULT, ADD)

        def finish(t, lo=0, hi=J):
            nc.vector.tensor_tensor(y[:, t, lo:hi], s[t][:, lo:hi], y[:, t, lo:hi], ADD)
            nc.sync.dma_start(out[P * t : P * (t + 1), lo:hi], y[:, t, lo:hi])

        features((0, 1), 0)
        features((0, 1), 1)
        features((2, 3), 0)
        features((2, 3), 1, copy=nc.vector.tensor_copy)
        y = keep.tile([P, TILES, J], F32, name="y", tag="raw20")
        for pair in ((0, 1), (2, 3)):
            for t in pair:
                first_tap(t)
            for lag in (1, 2):
                for t in pair:
                    add_tap(t, lag)
        for t in range(TILES):
            context(t)
        for t in (0, 1):
            aside = keep.tile([P, J], F32, name="aside%d" % t)
            nc.scalar.copy(aside[:], s[t][:])
            nc.gpsimd.tensor_tensor(y[:, t, :], y[:, t, :], aside[:], ADD)
            nc.scalar.dma_start(out[P * t : P * (t + 1), :], y[:, t, :])
        finish(2)
        finish(3, 0, J // 2)
        finish(3, J // 2, J)
